import numpy as np
CORES = [1,25,206]
N = 3
def setup_inputs(rng):
    return {"x": rng.standard_normal((N, 128, 16), dtype=np.float32)}
def reference(x):
    g = np.concatenate(list(x), axis=1)
    return {"y": np.broadcast_to(g, (N,) + g.shape)}

@@ -1,0 +1,58 @@
+from concourse.bass import DstId, RemoteDMATransfer
+
+SCRATCH = {
+    "gat": ("sbuf", [128, 48], "float32"),
+}
+SEMAPHORES = ["loaded", "sent", "arrived", "stored"]
+
+OFF = 0x00FF
+ON = 0xFF00
+
+
+def helper_of(core):
+    return (core // 8) * 8 + (2 if core % 8 < 4 else 6)
+
+
+def routes(T, topo):
+    out = {}
+    for i, s in enumerate(T.cores):
+        direct = [d for d in T.cores if d != s and topo.may_write(s, d)]
+        relayed = [d for d in T.cores if d != s and not topo.may_write(s, d)]
+        out[i] = (direct, relayed)
+    return out
+
+
+def transfer(T, topo, src_core, dsts, blk, mask):
+    ids = []
+    for d in dsts:
+        rid, pid = topo.addr(d, src_core)
+        ids.append(DstId(rid=rid, pnc=pid))
+    return RemoteDMATransfer(dst_ids=ids, dma_engine_mask=mask, remote_sem=T.sem.arrived,
+                             srcs=[T.gat[:, blk]], dsts=[T.gat[:, blk] for d in dsts])
+
+
+def rank_program(g, core, T, topo):
+    rt = routes(T, topo)
+    rank = T.rank_of(core)
+    if rank is None:
+        for i, s in enumerate(T.cores):
+            if rt[i][1] and helper_of(s) == core:
+                blk = slice(16 * i, 16 * i + 16)
+                g.wait_ge(T.sem.arrived, 8)
+                g.remote_dma_fused([transfer(T, topo, core, rt[i][1], blk, OFF)], local_sem=T.sem.sent)
+                g.wait_ge(T.sem.sent, 8)
+        return
+    blk = slice(16 * rank, 16 * rank + 16)
+    direct, relayed = rt[rank]
+    g.dma_start(T.gat[:, blk], T.x[:, :]).then_inc(T.sem.loaded, 16)
+    g.wait_ge(T.sem.loaded, 16)
+    trs = []
+    if relayed:
+        trs.append(transfer(T, topo, core, [helper_of(core)], blk, ON))
+    if direct:
+        trs.append(transfer(T, topo, core, direct, blk, OFF))
+    g.remote_dma_fused(trs, local_sem=T.sem.sent)
+    g.wait_ge(T.sem.arrived, 8 * (len(T.cores) - 1))
+    g.dma_start(T.y[:, :], T.gat[:, :]).then_inc(T.sem.stored, 16)
+    g.wait_ge(T.sem.sent, 8 * len(trs))
+    g.wait_ge(T.sem.stored, 16)

@@ -1,9 +1,9 @@
 from concourse.bass import DstId, RemoteDMATransfer
 
 SCRATCH = {
-    "gat": ("sbuf", [128, 48], "float32"),
+    "blk": ("dram", [3, 128, 16], "float32"),
 }
-SEMAPHORES = ["loaded", "sent", "arrived", "stored"]
+SEMAPHORES = ["loaded", "sent", "stored", "arr0", "arr1", "arr2"]
 
 OFF = 0x00FF
 ON = 0xFF00
@@ -22,37 +22,40 @@ def routes(T, topo):
     return out
 
 
-def transfer(T, topo, src_core, dsts, blk, mask):
+def transfer(T, topo, src_core, dsts, i, mask, sem):
     ids = []
     for d in dsts:
         rid, pid = topo.addr(d, src_core)
         ids.append(DstId(rid=rid, pnc=pid))
-    return RemoteDMATransfer(dst_ids=ids, dma_engine_mask=mask, remote_sem=T.sem.arrived,
-                             srcs=[T.gat[:, blk]], dsts=[T.gat[:, blk] for d in dsts])
+    return RemoteDMATransfer(dst_ids=ids, dma_engine_mask=mask, remote_sem=sem,
+                             srcs=[T.blk[i]], dsts=[T.blk[i] for d in dsts])
 
 
 def rank_program(g, core, T, topo):
     rt = routes(T, topo)
+    arr = [T.sem.arr0, T.sem.arr1, T.sem.arr2]
     rank = T.rank_of(core)
     if rank is None:
         for i, s in enumerate(T.cores):
             if rt[i][1] and helper_of(s) == core:
-                blk = slice(16 * i, 16 * i + 16)
-                g.wait_ge(T.sem.arrived, 8)
-                g.remote_dma_fused([transfer(T, topo, core, rt[i][1], blk, OFF)], local_sem=T.sem.sent)
+                g.wait_ge(arr[i], 8)
+                g.remote_dma_fused([transfer(T, topo, core, rt[i][1], i, OFF, arr[i])], local_sem=T.sem.sent)
                 g.wait_ge(T.sem.sent, 8)
         return
-    blk = slice(16 * rank, 16 * rank + 16)
     direct, relayed = rt[rank]
-    g.dma_start(T.gat[:, blk], T.x[:, :]).then_inc(T.sem.loaded, 16)
+    g.dma_start(T.blk[rank], T.x[:, :]).then_inc(T.sem.loaded, 16)
     g.wait_ge(T.sem.loaded, 16)
     trs = []
     if relayed:
-        trs.append(transfer(T, topo, core, [helper_of(core)], blk, ON))
+        trs.append(transfer(T, topo, core, [helper_of(core)], rank, ON, arr[rank]))
     if direct:
-        trs.append(transfer(T, topo, core, direct, blk, OFF))
+        trs.append(transfer(T, topo, core, direct, rank, OFF, arr[rank]))
     g.remote_dma_fused(trs, local_sem=T.sem.sent)
-    g.wait_ge(T.sem.arrived, 8 * (len(T.cores) - 1))
-    g.dma_start(T.y[:, :], T.gat[:, :]).then_inc(T.sem.stored, 16)
+    g.dma_start(T.y[:, 16 * rank:16 * rank + 16], T.x[:, :]).then_inc(T.sem.stored, 16)
+    others = [j for j in range(len(T.cores)) if j != rank]
+    others.sort(key=lambda j: 0 if core in rt[j][0] else 1)
+    for j in others:
+        g.wait_ge(arr[j], 8)
+        g.dma_start(T.y[:, 16 * j:16 * j + 16], T.blk[j]).then_inc(T.sem.stored, 16)
     g.wait_ge(T.sem.sent, 8 * len(trs))
-    g.wait_ge(T.sem.stored, 16)
+    g.wait_ge(T.sem.stored, 16 * len(T.cores))

@@ -5,19 +5,21 @@ SCRATCH = {
 }
 SEMAPHORES = ["loaded", "sent", "stored", "arr0", "arr1", "arr2"]
 
-OFF = 0x00FF
-ON = 0xFF00
+LOW = 0x00FF
 
 
-def helper_of(core):
-    return (core // 8) * 8 + (2 if core % 8 < 4 else 6)
+def helper_of(topo, src, dst):
+    return topo.host(dst) * 128 + (topo.chip(dst) ^ 1) * 8 + (2 if topo.die(src) == 1 else 6)
 
 
 def routes(T, topo):
     out = {}
     for i, s in enumerate(T.cores):
         direct = [d for d in T.cores if d != s and topo.may_write(s, d)]
-        relayed = [d for d in T.cores if d != s and not topo.may_write(s, d)]
+        relayed = {}
+        for d in T.cores:
+            if d != s and not topo.may_write(s, d):
+                relayed[helper_of(topo, s, d)] = d
         out[i] = (direct, relayed)
     return out
 
@@ -36,26 +38,21 @@ def rank_program(g, core, T, topo):
     arr = [T.sem.arr0, T.sem.arr1, T.sem.arr2]
     rank = T.rank_of(core)
     if rank is None:
-        for i, s in enumerate(T.cores):
-            if rt[i][1] and helper_of(s) == core:
+        for i in range(len(T.cores)):
+            if core in rt[i][1]:
                 g.wait_ge(arr[i], 8)
-                g.remote_dma_fused([transfer(T, topo, core, rt[i][1], i, OFF, arr[i])], local_sem=T.sem.sent)
+                g.remote_dma_fused([transfer(T, topo, core, [rt[i][1][core]], i, LOW, arr[i])], local_sem=T.sem.sent)
                 g.wait_ge(T.sem.sent, 8)
         return
     direct, relayed = rt[rank]
     g.dma_start(T.blk[rank], T.x[:, :]).then_inc(T.sem.loaded, 16)
     g.wait_ge(T.sem.loaded, 16)
-    trs = []
-    if relayed:
-        trs.append(transfer(T, topo, core, [helper_of(core)], rank, ON, arr[rank]))
-    if direct:
-        trs.append(transfer(T, topo, core, direct, rank, OFF, arr[rank]))
-    g.remote_dma_fused(trs, local_sem=T.sem.sent)
+    g.remote_dma_fused([transfer(T, topo, core, sorted(relayed) + direct, rank, LOW, arr[rank])], local_sem=T.sem.sent)
     g.dma_start(T.y[:, 16 * rank:16 * rank + 16], T.x[:, :]).then_inc(T.sem.stored, 16)
     others = [j for j in range(len(T.cores)) if j != rank]
     others.sort(key=lambda j: 0 if core in rt[j][0] else 1)
     for j in others:
         g.wait_ge(arr[j], 8)
         g.dma_start(T.y[:, 16 * j:16 * j + 16], T.blk[j]).then_inc(T.sem.stored, 16)
-    g.wait_ge(T.sem.sent, 8 * len(trs))
+    g.wait_ge(T.sem.sent, 8)
     g.wait_ge(T.sem.stored, 16 * len(T.cores))

from concourse.bass import DstId, RemoteDMATransfer

SCRATCH = {
    "blk": ("dram", [3, 128, 16], "float32"),
}
SEMAPHORES = ["loaded", "sent", "stored", "arr0", "arr1", "arr2"]

LOW = 0x00FF


def helper_of(topo, src, dst):
    return topo.host(dst) * 128 + (topo.chip(dst) ^ 1) * 8 + (2 if topo.die(src) == 1 else 6)


def routes(T, topo):
    out = {}
    for i, s in enumerate(T.cores):
        direct = [d for d in T.cores if d != s and topo.may_write(s, d)]
        relayed = {}
        for d in T.cores:
            if d != s and not topo.may_write(s, d):
                relayed[helper_of(topo, s, d)] = d
        out[i] = (direct, relayed)
    return out


def transfer(T, topo, src_core, dsts, i, mask, sem):
    ids = []
    for d in dsts:
        rid, pid = topo.addr(d, src_core)
        ids.append(DstId(rid=rid, pnc=pid))
    return RemoteDMATransfer(dst_ids=ids, dma_engine_mask=mask, remote_sem=sem,
                             srcs=[T.blk[i]], dsts=[T.blk[i] for d in dsts])


def rank_program(g, core, T, topo):
    rt = routes(T, topo)
    arr = [T.sem.arr0, T.sem.arr1, T.sem.arr2]
    rank = T.rank_of(core)
    if rank is None:
        for i in range(len(T.cores)):
            if core in rt[i][1]:
                g.wait_ge(arr[i], 8)
                g.remote_dma_fused([transfer(T, topo, core, [rt[i][1][core]], i, LOW, arr[i])], local_sem=T.sem.sent)
                g.wait_ge(T.sem.sent, 8)
        return
    direct, relayed = rt[rank]
    g.dma_start(T.blk[rank], T.x[:, :]).then_inc(T.sem.loaded, 16)
    g.wait_ge(T.sem.loaded, 16)
    g.remote_dma_fused([transfer(T, topo, core, sorted(relayed) + direct, rank, LOW, arr[rank])], local_sem=T.sem.sent)
    g.dma_start(T.y[:, 16 * rank:16 * rank + 16], T.x[:, :]).then_inc(T.sem.stored, 16)
    others = [j for j in range(len(T.cores)) if j != rank]
    others.sort(key=lambda j: 0 if core in rt[j][0] else 1)
    for j in others:
        g.wait_ge(arr[j], 8)
        g.dma_start(T.y[:, 16 * j:16 * j + 16], T.blk[j]).then_inc(T.sem.stored, 16)
    g.wait_ge(T.sem.sent, 8)
    g.wait_ge(T.sem.stored, 16 * len(T.cores))
